import numpy as np
import ml_dtypes


def mxq(x, axis, fmt="e4m3"):
    dtype, down = {"e4m3": (ml_dtypes.float8_e4m3fn, 7), "e5m2": (ml_dtypes.float8_e5m2, 14)}[fmt]
    v = np.moveaxis(np.asarray(x, np.float32).astype(ml_dtypes.bfloat16).astype(np.float64), axis, -1)
    blocks = v.reshape(v.shape[:-1] + (-1, 32))
    amax = np.abs(blocks).max(-1, keepdims=True)
    byte = np.maximum(np.where(amax > 0, np.frexp(amax)[1] - 1 + 127, 0) - down, 1)
    scale = np.exp2(byte - 127.0)
    codes = (blocks / scale).astype(np.float32).astype(dtype).astype(np.float64)
    return np.moveaxis((codes * scale).reshape(v.shape), -1, axis)


WIDE = False


def mx_kscale(k):
    if not WIDE:
        return np.ones(k)
    levels = np.array([10, -10, 5, -5, 0])
    if k % 512:
        return np.exp2(np.random.permutation(np.resize(levels, k // 32))).repeat(32)
    a = np.empty((k // 512, 16))
    for p in range(k // 512):
        a[p, :8] = np.random.permutation(np.resize(levels, 8))
        for g in range(8):
            far = levels[np.abs(levels - a[p, g]) >= 10]
            a[p, g + 8] = far[np.random.randint(len(far))]
    return np.exp2(a.ravel()).repeat(32)


def f64(x):
    return np.asarray(x).astype(np.float64)


def striped(idx):
    return np.tile(idx.reshape(-1, 16).T, (8, 1)).astype(np.uint16)


def unstriped(offs):
    return offs[:16].T.reshape(-1).astype(np.int64)


def striped8(idx):
    return np.concatenate([x.reshape(-1, 16).T for x in idx]).astype(np.uint16)


def runs(offs, k):
    lists = np.stack([offs[16 * r : 16 * r + 16].T.reshape(-1) for r in range(8)]).astype(np.int64)
    return lists[np.arange(k) % 512 // 64]


def pack_weight(w):
    k, n = w.shape
    w = f64(np.asarray(w, np.float32).astype(ml_dtypes.bfloat16)).reshape(k // 32, 32, n)
    amax = np.abs(w).max(1)
    byte = np.clip(np.where(amax > 0, np.frexp(amax)[1] - 1 + 127 - 7, 1), 1, 254)
    scaled = (w * np.exp2(127.0 - byte)[:, None, :]).reshape(k, n).astype(np.float32)
    words = np.ascontiguousarray(scaled.reshape(k // 512, 128, 4, n).transpose(0, 1, 3, 2)).astype(ml_dtypes.float8_e4m3fn).view(np.uint8)
    return words, np.ascontiguousarray(byte.astype(np.uint8).reshape(k // 512, 16, n))


def unpack_weight(words, scales):
    g, p, n, _ = words.shape
    vals = np.ascontiguousarray(words).view(ml_dtypes.float8_e4m3fn).astype(np.float64) * np.repeat(np.exp2(scales.astype(np.float64) - 127.0), 8, axis=1)[..., None]
    return vals.transpose(0, 1, 3, 2).reshape(g * 512, n)


def sigmoid(v):
    return 1.0 / (1.0 + np.exp(-np.maximum(v, -700.0)))


K, T, S, N, H, W = 512, 2048, 512, 512, 512, 1024


def setup_inputs():
    n = np.random.standard_normal
    s = mx_kscale(K)[:, None]
    u = mx_kscale(S)
    packed_xT = pack_weight(n((K, T)) * s)
    return {
        "x_words": packed_xT[0],
        "x_scales": packed_xT[1],
        "wa": (n((K, H)) / np.sqrt(K) / s).astype(np.float32),
        "tau": np.random.uniform(0.2, 0.6, (S, 1)).astype(np.float32),
        "tau2": np.random.uniform(0.6, 1.0, (S, 1)).astype(np.float32),
        "gt": (np.random.uniform(0.5, 1.5, (S, 1)) * u[:, None]).astype(np.float32),
        "w1": (n((S, N)) / np.sqrt(S) / u[:, None]).astype(np.float32),
        "offs": striped(np.random.permutation(T)[:S]),
        "n1": striped8(np.stack([np.random.permutation(H) for _ in range(8)])),
        "n2": striped8(np.stack([np.random.permutation(H) for _ in range(8)])),
        "n3": striped(np.random.randint(0, H, W)),
    }


def reference(x_words, x_scales, wa, tau, tau2, gt, w1, offs, n1, n2, n3):
    xq = unpack_weight(x_words, x_scales)[:, unstriped(offs)]
    y = xq.T @ mxq(f64(wa), 0, "e4m3")
    top = y.max(axis=1, keepdims=True)
    ea = np.exp(f64(tau) * (y[np.arange(S)[:, None], runs(n1, S)] - top))
    ea2 = np.exp(f64(tau2) * (y[np.arange(S)[:, None], runs(n2, S)] - top))
    z = f64(gt) * (3.0 * (ea - ea2))
    h = mxq(f64(w1), 0, "e4m3").T @ mxq(z, 0, "e4m3")
    mb = h[:, unstriped(n3)]
    mn = mb.reshape(N, H, 2).min(axis=2)
    mx = mb.reshape(N, H, 2).max(axis=2)
    return (h - mn) * sigmoid(mx)

@@ -1,0 +1,212 @@
+from contextlib import ExitStack
+
+import concourse.mybir as mybir
+
+K, T, S, N, H, W = 512, 2048, 512, 512, 512, 1024
+FLOPS = 2 * K * S * H + 2 * S * N * H
+
+F32 = mybir.dt.float32
+BF16 = mybir.dt.bfloat16
+I32 = mybir.dt.int32
+U32 = mybir.dt.uint32
+U16 = mybir.dt.uint16
+U8 = mybir.dt.uint8
+FP8X4 = mybir.dt.float8_e4m3fn_x4
+ALU = mybir.AluOpType
+ACT = mybir.ActivationFunctionType
+
+P = 128
+PACK = 4
+STRIPE = 16
+HALF = 256
+SPARE = 32
+Z_PIECES = ((0, 256), (256, 128), (384, 128))
+
+
+def tile_picked_toketwghard_none_p_kernel(tc, x_words, x_scales, wa, tau, tau2, gt, w1, offs, n1, n2, n3, out):
+    nc = tc.nc
+    with ExitStack() as ctx:
+        keep = ctx.enter_context(tc.tile_pool(name="keep", bufs=1))
+        psum = ctx.enter_context(tc.psum_pool(name="psum", bufs=1))
+
+        offs_sb = keep.tile([P, S // STRIPE], U16, name="offs_sb")
+        n1_sb = keep.tile([P, H // STRIPE], U16, name="n1_sb")
+        n2_sb = keep.tile([P, H // STRIPE], U16, name="n2_sb")
+        n3_sb = keep.tile([P, W // STRIPE], U16, name="n3_sb")
+        x_table = keep.tile([P, T], U32, name="x_table")
+        scale_table = keep.tile([P, T], U8, name="scale_table")
+        wa_raw = [keep.tile([P, PACK, HALF], F32, name="wa_raw%d" % c) for c in range(2)]
+        w1_raw = [keep.tile([P, PACK, HALF], F32, name="w1_raw%d" % c, tag="w1_raw%d" % c) for c in range(2)]
+        rates = keep.tile([P, 2, 8], F32, name="rates")
+        gate = keep.tile([P, PACK], F32, name="gate")
+        h_half = [keep.tile([P, H + SPARE], F32, name="h_half%d" % m) for m in range(4)]
+
+        nc.vector.memset(scale_table[:].bitcast(I32), 0)
+        nc.sync.dma_start(offs_sb[:], offs)
+        wa_rows = wa.rearrange("(p j) w -> p j w", j=PACK)
+        w1_rows = w1.rearrange("(p j) w -> p j w", j=PACK)
+        nc.sync.dma_start(wa_raw[0][:], wa_rows[:, :, 0:HALF])
+        for q in range(4):
+            nc.sync.dma_start(
+                scale_table[32 * q : 32 * q + 4, :].bitcast(I32), x_scales[0, 4 * q : 4 * q + 4, :].bitcast(I32)
+            )
+        nc.sync.dma_start(wa_raw[1][:], wa_rows[:, :, HALF:])
+        nc.sync.dma_start(x_table[:].bitcast(I32), x_words[0].rearrange("p c r -> p (c r)").bitcast(I32))
+        nc.sync.dma_start(n2_sb[:], n2)
+        nc.sync.dma_start(n1_sb[:], n1)
+        nc.sync.dma_start(rates[:, 1, 0:PACK], tau2.rearrange("(p t) o -> p (t o)", t=PACK))
+        nc.sync.dma_start(rates[:, 0, 0:PACK], tau.rearrange("(p t) o -> p (t o)", t=PACK))
+        nc.sync.dma_start(gate[:], gt.rearrange("(p t) o -> p (t o)", t=PACK))
+        for c in range(2):
+            nc.sync.dma_start(w1_raw[c][:], w1_rows[:, :, c * HALF : (c + 1) * HALF])
+        nc.sync.dma_start(n3_sb[:], n3)
+        for m in range(4):
+            nc.vector.memset(h_half[m][:, H:], 0.0)
+
+        x_codes = keep.tile([P, PACK, P], U32, name="x_codes", align_bytes=64)
+        x_bytes = keep.tile([P, PACK, P], U8, name="x_bytes", align_bytes=64)
+        nc.vector.tensor_copy(x_bytes[:].rearrange("p t m -> p m t"), scale_table[:].indirect(offs_sb[:]))
+
+        gate3 = keep.tile([P, PACK], F32, name="gate3")
+        nc.gpsimd.tensor_scalar(gate3[:], gate[:], 3.0, 0.0, ALU.mult, ALU.add)
+
+        def interleave(on_scalar, raw, name):
+            width = raw.shape[2]
+            grouped = keep.tile([P, width, PACK], BF16, name=name, align_bytes=64)
+            if on_scalar:
+                nc.scalar.activation(grouped[:], raw.rearrange("p j w -> p w j"), ACT.Copy)
+            else:
+                nc.vector.tensor_copy(grouped[:], raw.rearrange("p j w -> p w j"))
+            return grouped
+
+        def quantize(grouped, name):
+            width = grouped.shape[1]
+            codes = keep.tile([P, width], U32, name=name + "_codes", align_bytes=64)
+            scales = keep.tile([P, width], U8, name=name + "_scales", align_bytes=64)
+            nc.vector.quantize_mx(
+                out=codes[:].bitcast(FP8X4), scales=scales[:], in_=grouped[:].rearrange("p w j -> p (w j)")
+            )
+            return codes, scales
+
+        wa_grouped = [interleave(c == 0, wa_raw[c][:], "wa_grouped%d" % c) for c in range(2)]
+        wa_mx = [quantize(wa_grouped[c], "wa%d" % c) for c in range(2)]
+        nc.vector.tensor_copy(x_codes[:].rearrange("p t m -> p m t"), x_table[:].indirect(offs_sb[:]))
+        w1_grouped0 = interleave(True, w1_raw[0][:], "w1_grouped0")
+
+        y_sb, bias = [], []
+        for t in range(PACK):
+            acc = psum.tile([P, H], F32, name="y_acc%d" % t, tag="bank%d" % t)
+            for c in range(2):
+                nc.tensor.matmul_mx(
+                    out=acc[:, c * HALF : (c + 1) * HALF],
+                    lhsT=x_codes[:, t, :].bitcast(FP8X4),
+                    lhsT_scale=x_bytes[:, t, :],
+                    rhs=wa_mx[c][0][:].bitcast(FP8X4),
+                    rhs_scale=wa_mx[c][1][:],
+                    start=True,
+                    stop=True,
+                )
+            y_t = keep.tile([P, H], F32, name="y%d" % t)
+            top = keep.tile([P, 1], F32, name="top%d" % t)
+            bias_t = keep.tile([P, 2], F32, name="bias%d" % t)
+            nc.vector.tensor_scalar(y_t[:], acc[:], 1.0, None, ALU.mult, ALU.max, accum_out=top[:])
+            nc.gpsimd.tensor_scalar(bias_t[:], rates[:, :, t], top[:], -1.0, ALU.mult, ALU.mult)
+            y_sb.append(y_t)
+            bias.append(bias_t)
+
+        w1_mx = []
+        free_banks = [4, 5, 6, 7, 0, 1, 2]
+        for piece, (first, width) in enumerate(Z_PIECES):
+            entries = slice(first // STRIPE, (first + width) // STRIPE)
+            z = keep.tile([P, PACK, width], F32, name="z%d" % piece)
+            for t in range(PACK):
+                ea = keep.tile([P, width], F32, name="ea%d_%d" % (piece, t))
+                ea2_tag = "w1_raw0" if (piece, t) == (0, 0) else "ea2%d_%d" % (piece, t)
+                ea2 = keep.tile([P, width], F32, name="ea2%d_%d" % (piece, t), tag=ea2_tag)
+                scaled = keep.tile([P, width], F32, name="scaled%d_%d" % (piece, t))
+                nc.scalar.activation(
+                    ea2[:], y_sb[t][:].indirect(n2_sb[:, entries]), ACT.Exp,
+                    bias=bias[t][:, 1:2], scale=rates[:, 1, t : t + 1],
+                )
+                nc.scalar.activation(
+                    ea[:], y_sb[t][:].indirect(n1_sb[:, entries]), ACT.Exp,
+                    bias=bias[t][:, 0:1], scale=rates[:, 0, t : t + 1],
+                )
+                nc.vector.tensor_scalar(scaled[:], ea2[:], gate3[:, t : t + 1], None, ALU.mult)
+                nc.vector.scalar_tensor_tensor(
+                    z[:, t, :], ea[:], gate3[:, t : t + 1], scaled[:], ALU.mult, ALU.subtract
+                )
+            z_grouped = interleave(False, z[:], "z_grouped%d" % piece)
+            if piece == 0:
+                w1_mx.append(quantize(w1_grouped0, "w1_0"))
+            z_codes, z_scales = quantize(z_grouped, "z%d" % piece)
+            if piece == 0:
+                w1_mx.append(quantize(interleave(False, w1_raw[1][:], "w1_grouped1"), "w1_1"))
+            last = piece == len(Z_PIECES) - 1
+            per_bank = 1 if last else H // width
+            accs = []
+            for m in range(4):
+                if m % per_bank == 0:
+                    bank = psum.tile(
+                        [P, per_bank, width], F32, name="h_acc%d_%d" % (piece, m), tag="bank%d" % free_banks.pop(0)
+                    )
+                cols = slice((m % 2) * P, (m % 2 + 1) * P)
+                nc.tensor.matmul_mx(
+                    out=bank[:, m % per_bank, :],
+                    lhsT=w1_mx[m // 2][0][:, cols].bitcast(FP8X4),
+                    lhsT_scale=w1_mx[m // 2][1][:, cols],
+                    rhs=z_codes[:].bitcast(FP8X4),
+                    rhs_scale=z_scales[:],
+                    start=True,
+                    stop=True,
+                )
+                accs.append(bank[:, m % per_bank, :])
+            if piece == 0:
+                held = []
+            held.append((first, width, accs))
+
+        for piece, (first, width, accs) in enumerate(held):
+            for m in range(4):
+                target = h_half[m][:, first : first + width]
+                if piece == len(held) - 1 and m % 2 == 0:
+                    nc.vector.tensor_scalar(target, accs[m], 0.5, None, ALU.mult)
+                else:
+                    nc.scalar.activation(target, accs[m], ACT.Copy, scale=0.5)
+
+        units = [(m, c) for m in range(4) for c in range(2)]
+
+        def fetch(u):
+            m, c = units[u]
+            members = keep.tile([P, HALF, 2], F32, name="members%d" % u)
+            window = h_half[m][:].indirect(n3_sb[:, c * 32 : (c + 1) * 32])
+            flat = members[:].rearrange("p j e -> p (j e)")
+            if u == 0:
+                nc.vector.tensor_copy(flat, window)
+            else:
+                nc.scalar.activation(flat, window, ACT.Copy)
+            return members
+
+        def finish(u, gap, curve):
+            m, c = units[u]
+            result = keep.tile([P, HALF], F32, name="result%d" % u)
+            nc.vector.scalar_tensor_tensor(result[:], curve[:], 1.0, gap[:], ALU.add, ALU.mult)
+            nc.sync.dma_start(out[m * P : (m + 1) * P, c * HALF : (c + 1) * HALF], result[:])
+
+        fetched = [fetch(0), fetch(1)]
+        pending = None
+        for u, (m, c) in enumerate(units):
+            members = fetched[u]
+            larger = keep.tile([P, HALF], F32, name="larger%d" % u)
+            smaller = keep.tile([P, HALF], F32, name="smaller%d" % u)
+            gap = keep.tile([P, HALF], F32, name="gap%d" % u)
+            curve = keep.tile([P, HALF], F32, name="curve%d" % u)
+            nc.vector.tensor_tensor(larger[:], members[:, :, 0], members[:, :, 1], ALU.max)
+            nc.vector.tensor_tensor(smaller[:], members[:, :, 0], members[:, :, 1], ALU.min)
+            nc.scalar.activation(curve[:], larger[:], ACT.Tanh)
+            if u + 2 < len(units):
+                fetched.append(fetch(u + 2))
+            if pending is not None:
+                finish(*pending)
+            nc.vector.tensor_tensor(gap[:], h_half[m][:, c * HALF : (c + 1) * HALF], smaller[:], ALU.subtract)
+            pending = (u, gap, curve)
+        finish(*pending)

@@ -19,8 +19,7 @@ P = 128
 PACK = 4
 STRIPE = 16
 HALF = 256
-SPARE = 32
-Z_PIECES = ((0, 256), (256, 128), (384, 128))
+WHOLE_ROWS = 2
 
 
 def tile_picked_toketwghard_none_p_kernel(tc, x_words, x_scales, wa, tau, tau2, gt, w1, offs, n1, n2, n3, out):
@@ -39,45 +38,33 @@ def tile_picked_toketwghard_none_p_kernel(tc, x_words, x_scales, wa, tau, tau2, 
         w1_raw = [keep.tile([P, PACK, HALF], F32, name="w1_raw%d" % c, tag="w1_raw%d" % c) for c in range(2)]
         rates = keep.tile([P, 2, 8], F32, name="rates")
         gate = keep.tile([P, PACK], F32, name="gate")
-        h_half = [keep.tile([P, H + SPARE], F32, name="h_half%d" % m) for m in range(4)]
+        y_sb = [keep.tile([P, 2 * H if t < WHOLE_ROWS else H], F32, name="y%d" % t) for t in range(PACK)]
+        h_spare = [32, W - H + 32, W - H + 32, 32]
+        h_half = [keep.tile([P, H + h_spare[m]], F32, name="h_half%d" % m) for m in range(4)]
 
-        nc.vector.memset(scale_table[:].bitcast(I32), 0)
-        nc.sync.dma_start(offs_sb[:], offs)
         wa_rows = wa.rearrange("(p j) w -> p j w", j=PACK)
         w1_rows = w1.rearrange("(p j) w -> p j w", j=PACK)
+        nc.vector.memset(scale_table[:].bitcast(I32), 0)
+        nc.sync.dma_start(offs_sb[:], offs)
         nc.sync.dma_start(wa_raw[0][:], wa_rows[:, :, 0:HALF])
         for q in range(4):
             nc.sync.dma_start(
                 scale_table[32 * q : 32 * q + 4, :].bitcast(I32), x_scales[0, 4 * q : 4 * q + 4, :].bitcast(I32)
             )
-        nc.sync.dma_start(wa_raw[1][:], wa_rows[:, :, HALF:])
         nc.sync.dma_start(x_table[:].bitcast(I32), x_words[0].rearrange("p c r -> p (c r)").bitcast(I32))
+        nc.sync.dma_start(wa_raw[1][:], wa_rows[:, :, HALF:])
+        nc.sync.dma_start(w1_raw[0][:], w1_rows[:, :, 0:HALF])
         nc.sync.dma_start(n2_sb[:], n2)
         nc.sync.dma_start(n1_sb[:], n1)
         nc.sync.dma_start(rates[:, 1, 0:PACK], tau2.rearrange("(p t) o -> p (t o)", t=PACK))
         nc.sync.dma_start(rates[:, 0, 0:PACK], tau.rearrange("(p t) o -> p (t o)", t=PACK))
         nc.sync.dma_start(gate[:], gt.rearrange("(p t) o -> p (t o)", t=PACK))
-        for c in range(2):
-            nc.sync.dma_start(w1_raw[c][:], w1_rows[:, :, c * HALF : (c + 1) * HALF])
+        nc.sync.dma_start(w1_raw[1][:], w1_rows[:, :, HALF:])
         nc.sync.dma_start(n3_sb[:], n3)
+        for t in range(WHOLE_ROWS):
+            nc.vector.memset(y_sb[t][:, H:], 0.0)
         for m in range(4):
             nc.vector.memset(h_half[m][:, H:], 0.0)
-
-        x_codes = keep.tile([P, PACK, P], U32, name="x_codes", align_bytes=64)
-        x_bytes = keep.tile([P, PACK, P], U8, name="x_bytes", align_bytes=64)
-        nc.vector.tensor_copy(x_bytes[:].rearrange("p t m -> p m t"), scale_table[:].indirect(offs_sb[:]))
-
-        gate3 = keep.tile([P, PACK], F32, name="gate3")
-        nc.gpsimd.tensor_scalar(gate3[:], gate[:], 3.0, 0.0, ALU.mult, ALU.add)
-
-        def interleave(on_scalar, raw, name):
-            width = raw.shape[2]
-            grouped = keep.tile([P, width, PACK], BF16, name=name, align_bytes=64)
-            if on_scalar:
-                nc.scalar.activation(grouped[:], raw.rearrange("p j w -> p w j"), ACT.Copy)
-            else:
-                nc.vector.tensor_copy(grouped[:], raw.rearrange("p j w -> p w j"))
-            return grouped
 
         def quantize(grouped, name):
             width = grouped.shape[1]
@@ -88,125 +75,167 @@ def tile_picked_toketwghard_none_p_kernel(tc, x_words, x_scales, wa, tau, tau2, 
             )
             return codes, scales
 
-        wa_grouped = [interleave(c == 0, wa_raw[c][:], "wa_grouped%d" % c) for c in range(2)]
-        wa_mx = [quantize(wa_grouped[c], "wa%d" % c) for c in range(2)]
+        x_codes = keep.tile([P, PACK, P], U32, name="x_codes", align_bytes=64)
+        x_bytes = keep.tile([P, PACK, P], U8, name="x_bytes", align_bytes=64)
+        wa_grouped = [keep.tile([P, HALF, PACK], BF16, name="wa_grouped%d" % c, tag="wa_grouped%d" % c, align_bytes=64) for c in range(2)]
+        w1_grouped = keep.tile([P, N, PACK], BF16, name="w1_grouped", align_bytes=64)
+        nc.scalar.activation(wa_grouped[0][:], wa_raw[0][:].rearrange("p j w -> p w j"), ACT.Copy)
+        nc.vector.tensor_copy(x_bytes[:].rearrange("p t m -> p m t"), scale_table[:].indirect(offs_sb[:]))
+        wa_mx = [quantize(wa_grouped[0], "wa0")]
         nc.vector.tensor_copy(x_codes[:].rearrange("p t m -> p m t"), x_table[:].indirect(offs_sb[:]))
-        w1_grouped0 = interleave(True, w1_raw[0][:], "w1_grouped0")
+        late = wa_raw[1][:].rearrange("p j w -> p w j")
+        nc.scalar.activation(wa_grouped[1][:, 0:P, :], late[:, 0:P, :], ACT.Copy)
+        nc.vector.tensor_copy(wa_grouped[1][:, P:, :], late[:, P:, :])
+        wa_mx.append(quantize(wa_grouped[1], "wa1"))
+        nc.scalar.activation(w1_grouped[:, 0:HALF, :], w1_raw[0][:].rearrange("p j w -> p w j"), ACT.Copy)
 
-        y_sb, bias = [], []
+        def project(acc, t, c):
+            nc.tensor.matmul_mx(
+                out=acc,
+                lhsT=x_codes[:, t, :].bitcast(FP8X4),
+                lhsT_scale=x_bytes[:, t, :],
+                rhs=wa_mx[c][0][:].bitcast(FP8X4),
+                rhs_scale=wa_mx[c][1][:],
+                start=True,
+                stop=True,
+            )
+
+        bias = []
         for t in range(PACK):
-            acc = psum.tile([P, H], F32, name="y_acc%d" % t, tag="bank%d" % t)
-            for c in range(2):
-                nc.tensor.matmul_mx(
-                    out=acc[:, c * HALF : (c + 1) * HALF],
-                    lhsT=x_codes[:, t, :].bitcast(FP8X4),
-                    lhsT_scale=x_bytes[:, t, :],
-                    rhs=wa_mx[c][0][:].bitcast(FP8X4),
-                    rhs_scale=wa_mx[c][1][:],
-                    start=True,
-                    stop=True,
-                )
-            y_t = keep.tile([P, H], F32, name="y%d" % t)
             top = keep.tile([P, 1], F32, name="top%d" % t)
             bias_t = keep.tile([P, 2], F32, name="bias%d" % t)
-            nc.vector.tensor_scalar(y_t[:], acc[:], 1.0, None, ALU.mult, ALU.max, accum_out=top[:])
+            if t == 0:
+                early_top = keep.tile([P, 1], F32, name="early_top", tag="wa_grouped1", align_bytes=64)
+                early = psum.tile([P, HALF], F32, name="y_acc_early", tag="bank4")
+                acc = psum.tile([P, HALF], F32, name="y_acc0", tag="bank0")
+                project(early[:], 0, 0)
+                project(acc[:], 0, 1)
+                nc.vector.tensor_scalar(
+                    y_sb[0][:, 0:HALF], early[:], 1.0, None, ALU.mult, ALU.max, accum_out=early_top[:]
+                )
+                nc.vector.tensor_scalar(
+                    y_sb[0][:, HALF:H], acc[:], 1.0, early_top[:], ALU.mult, ALU.max, accum_out=top[:]
+                )
+            else:
+                acc = psum.tile([P, H], F32, name="y_acc%d" % t, tag="bank%d" % t)
+                for c in range(2):
+                    project(acc[:, c * HALF : (c + 1) * HALF], t, c)
+                nc.vector.tensor_scalar(y_sb[t][:, 0:H], acc[:], 1.0, None, ALU.mult, ALU.max, accum_out=top[:])
             nc.gpsimd.tensor_scalar(bias_t[:], rates[:, :, t], top[:], -1.0, ALU.mult, ALU.mult)
-            y_sb.append(y_t)
             bias.append(bias_t)
 
-        w1_mx = []
-        free_banks = [4, 5, 6, 7, 0, 1, 2]
-        for piece, (first, width) in enumerate(Z_PIECES):
+        gate3 = keep.tile([P, PACK], F32, name="gate3")
+        nc.gpsimd.tensor_scalar(gate3[:], gate[:], 3.0, 0.0, ALU.mult, ALU.add)
+        nc.vector.tensor_copy(w1_grouped[:, HALF:, :], w1_raw[1][:].rearrange("p j w -> p w j"))
+        w1_codes, w1_scales = quantize(w1_grouped, "w1")
+
+        z = keep.tile([P, 2, PACK, HALF], F32, name="z")
+
+        def make_z(t, first, width):
             entries = slice(first // STRIPE, (first + width) // STRIPE)
-            z = keep.tile([P, PACK, width], F32, name="z%d" % piece)
-            for t in range(PACK):
-                ea = keep.tile([P, width], F32, name="ea%d_%d" % (piece, t))
-                ea2_tag = "w1_raw0" if (piece, t) == (0, 0) else "ea2%d_%d" % (piece, t)
-                ea2 = keep.tile([P, width], F32, name="ea2%d_%d" % (piece, t), tag=ea2_tag)
-                scaled = keep.tile([P, width], F32, name="scaled%d_%d" % (piece, t))
+            label = "%d_%d" % (t, first)
+            both = keep.tile([P, 2, width], F32, name="exp" + label, tag="w1_raw0" if t == 0 else "exp" + label)
+            scaled_tag = {(2, HALF): "scaled3_0", (3, HALF): "z_grouped0"}.get((t, first), "scaled" + label)
+            scaled = keep.tile([P, width], F32, name="scaled" + label, tag=scaled_tag, align_bytes=64)
+            for which, lists in ((1, n2_sb), (0, n1_sb)):
                 nc.scalar.activation(
-                    ea2[:], y_sb[t][:].indirect(n2_sb[:, entries]), ACT.Exp,
-                    bias=bias[t][:, 1:2], scale=rates[:, 1, t : t + 1],
+                    both[:, which, :], y_sb[t][:].indirect(lists[:, entries]), ACT.Exp,
+                    bias=bias[t][:, which : which + 1], scale=rates[:, which, t : t + 1],
                 )
-                nc.scalar.activation(
-                    ea[:], y_sb[t][:].indirect(n1_sb[:, entries]), ACT.Exp,
-                    bias=bias[t][:, 0:1], scale=rates[:, 0, t : t + 1],
-                )
-                nc.vector.tensor_scalar(scaled[:], ea2[:], gate3[:, t : t + 1], None, ALU.mult)
-                nc.vector.scalar_tensor_tensor(
-                    z[:, t, :], ea[:], gate3[:, t : t + 1], scaled[:], ALU.mult, ALU.subtract
-                )
-            z_grouped = interleave(False, z[:], "z_grouped%d" % piece)
-            if piece == 0:
-                w1_mx.append(quantize(w1_grouped0, "w1_0"))
-            z_codes, z_scales = quantize(z_grouped, "z%d" % piece)
-            if piece == 0:
-                w1_mx.append(quantize(interleave(False, w1_raw[1][:], "w1_grouped1"), "w1_1"))
-            last = piece == len(Z_PIECES) - 1
-            per_bank = 1 if last else H // width
-            accs = []
+            nc.vector.tensor_scalar(scaled[:], both[:, 1, :], gate3[:, t : t + 1], None, ALU.mult)
+            nc.vector.scalar_tensor_tensor(
+                z[:, first // HALF : (first + width) // HALF, t, :],
+                both[:, 0, :].rearrange("p (c j) -> p c j", j=HALF),
+                gate3[:, t : t + 1],
+                scaled[:].rearrange("p (c j) -> p c j", j=HALF),
+                ALU.mult,
+                ALU.subtract,
+            )
+
+        for t in range(WHOLE_ROWS):
+            make_z(t, 0, H)
+        h_acc = {}
+        for c in range(2):
+            for t in range(WHOLE_ROWS, PACK):
+                make_z(t, c * HALF, HALF)
+            z_grouped = keep.tile([P, HALF, PACK], BF16, name="z_grouped%d" % c, tag="z_grouped%d" % c, align_bytes=64)
+            nc.vector.tensor_copy(z_grouped[:], z[:, c, :, :].rearrange("p t j -> p j t"))
+            z_codes, z_scales = quantize(z_grouped, "z%d" % c)
             for m in range(4):
-                if m % per_bank == 0:
-                    bank = psum.tile(
-                        [P, per_bank, width], F32, name="h_acc%d_%d" % (piece, m), tag="bank%d" % free_banks.pop(0)
-                    )
-                cols = slice((m % 2) * P, (m % 2 + 1) * P)
+                acc = psum.tile([P, HALF], F32, name="h_acc%d_%d" % (c, m), tag="bank%d" % ((5 + 4 * c + m) % 8))
                 nc.tensor.matmul_mx(
-                    out=bank[:, m % per_bank, :],
-                    lhsT=w1_mx[m // 2][0][:, cols].bitcast(FP8X4),
-                    lhsT_scale=w1_mx[m // 2][1][:, cols],
+                    out=acc[:],
+                    lhsT=w1_codes[:, m * P : (m + 1) * P].bitcast(FP8X4),
+                    lhsT_scale=w1_scales[:, m * P : (m + 1) * P],
                     rhs=z_codes[:].bitcast(FP8X4),
                     rhs_scale=z_scales[:],
                     start=True,
                     stop=True,
                 )
-                accs.append(bank[:, m % per_bank, :])
-            if piece == 0:
-                held = []
-            held.append((first, width, accs))
+                h_acc[c, m] = acc
 
-        for piece, (first, width, accs) in enumerate(held):
-            for m in range(4):
-                target = h_half[m][:, first : first + width]
-                if piece == len(held) - 1 and m % 2 == 0:
-                    nc.vector.tensor_scalar(target, accs[m], 0.5, None, ALU.mult)
-                else:
-                    nc.scalar.activation(target, accs[m], ACT.Copy, scale=0.5)
-
-        units = [(m, c) for m in range(4) for c in range(2)]
-
-        def fetch(u):
-            m, c = units[u]
-            members = keep.tile([P, HALF, 2], F32, name="members%d" % u)
-            window = h_half[m][:].indirect(n3_sb[:, c * 32 : (c + 1) * 32])
-            flat = members[:].rearrange("p j e -> p (j e)")
-            if u == 0:
-                nc.vector.tensor_copy(flat, window)
+        def leave_psum(on_scalar, c, m):
+            target = h_half[m][:, c * HALF : (c + 1) * HALF]
+            if on_scalar:
+                nc.scalar.activation(target, h_acc[c, m][:], ACT.Copy, scale=0.5)
             else:
+                nc.vector.tensor_scalar(target, h_acc[c, m][:], 0.5, None, ALU.mult)
+
+        members = [keep.tile([P, H, 2], F32, name="members%d" % m) for m in range(4)]
+        larger = [keep.tile([P, H], F32, name="larger%d" % m) for m in range(4)]
+        smaller = [keep.tile([P, H], F32, name="smaller%d" % m) for m in range(4)]
+        gap = [keep.tile([P, H], F32, name="gap%d" % m) for m in range(4)]
+        curve = [keep.tile([P, H], F32, name="curve%d" % m) for m in range(4)]
+        result = [keep.tile([P, H], F32, name="result%d" % m) for m in range(4)]
+
+        def fetch(on_scalar, m, cols):
+            window = h_half[m][:].indirect(n3_sb[:, 2 * cols.start // STRIPE : 2 * cols.stop // STRIPE])
+            flat = members[m][:, cols, :].rearrange("p j e -> p (j e)")
+            if on_scalar:
                 nc.scalar.activation(flat, window, ACT.Copy)
-            return members
+            else:
+                nc.vector.tensor_copy(flat, window)
 
-        def finish(u, gap, curve):
-            m, c = units[u]
-            result = keep.tile([P, HALF], F32, name="result%d" % u)
-            nc.vector.scalar_tensor_tensor(result[:], curve[:], 1.0, gap[:], ALU.add, ALU.mult)
-            nc.sync.dma_start(out[m * P : (m + 1) * P, c * HALF : (c + 1) * HALF], result[:])
+        def compare(m, cols):
+            pair = members[m]
+            nc.vector.tensor_tensor(smaller[m][:, cols], pair[:, cols, 0], pair[:, cols, 1], ALU.min)
+            nc.vector.tensor_tensor(larger[m][:, cols], pair[:, cols, 0], pair[:, cols, 1], ALU.max)
+            nc.vector.tensor_tensor(gap[m][:, cols], h_half[m][:, cols], smaller[m][:, cols], ALU.subtract)
 
-        fetched = [fetch(0), fetch(1)]
-        pending = None
-        for u, (m, c) in enumerate(units):
-            members = fetched[u]
-            larger = keep.tile([P, HALF], F32, name="larger%d" % u)
-            smaller = keep.tile([P, HALF], F32, name="smaller%d" % u)
-            gap = keep.tile([P, HALF], F32, name="gap%d" % u)
-            curve = keep.tile([P, HALF], F32, name="curve%d" % u)
-            nc.vector.tensor_tensor(larger[:], members[:, :, 0], members[:, :, 1], ALU.max)
-            nc.vector.tensor_tensor(smaller[:], members[:, :, 0], members[:, :, 1], ALU.min)
-            nc.scalar.activation(curve[:], larger[:], ACT.Tanh)
-            if u + 2 < len(units):
-                fetched.append(fetch(u + 2))
-            if pending is not None:
-                finish(*pending)
-            nc.vector.tensor_tensor(gap[:], h_half[m][:, c * HALF : (c + 1) * HALF], smaller[:], ALU.subtract)
-            pending = (u, gap, curve)
-        finish(*pending)
+        def bend(m, cols):
+            nc.scalar.activation(curve[m][:, cols], larger[m][:, cols], ACT.Tanh)
+
+        def finish(m, cols):
+            nc.vector.scalar_tensor_tensor(
+                result[m][:, cols], curve[m][:, cols], 1.0, gap[m][:, cols], ALU.add, ALU.mult
+            )
+            nc.sync.dma_start(out[m * P : (m + 1) * P, cols], result[m][:, cols])
+
+        left, right, whole = slice(0, HALF), slice(HALF, H), slice(0, H)
+        for m in range(4):
+            leave_psum(True, 0, m)
+        leave_psum(False, 1, 0)
+        leave_psum(True, 1, 1)
+        fetch(False, 0, left)
+        fetch(True, 0, right)
+        fetch(True, 1, whole)
+        leave_psum(False, 1, 2)
+        leave_psum(False, 1, 3)
+        fetch(True, 2, whole)
+        compare(0, whole)
+        bend(0, whole)
+        fetch(True, 3, left)
+        fetch(True, 3, right)
+        compare(1, whole)
+        bend(1, whole)
+        compare(2, whole)
+        bend(2, whole)
+        finish(0, whole)
+        compare(3, left)
+        bend(3, left)
+        compare(3, right)
+        bend(3, right)
+        finish(1, whole)
+        finish(2, whole)
+        finish(3, left)
+        finish(3, right)

@@ -19,7 +19,8 @@ P = 128
 PACK = 4
 STRIPE = 16
 HALF = 256
-WHOLE_ROWS = 2
+QUARTER = 128
+RUN = 4
 
 
 def tile_picked_toketwghard_none_p_kernel(tc, x_words, x_scales, wa, tau, tau2, gt, w1, offs, n1, n2, n3, out):
@@ -38,7 +39,7 @@ def tile_picked_toketwghard_none_p_kernel(tc, x_words, x_scales, wa, tau, tau2, 
         w1_raw = [keep.tile([P, PACK, HALF], F32, name="w1_raw%d" % c, tag="w1_raw%d" % c) for c in range(2)]
         rates = keep.tile([P, 2, 8], F32, name="rates")
         gate = keep.tile([P, PACK], F32, name="gate")
-        y_sb = [keep.tile([P, 2 * H if t < WHOLE_ROWS else H], F32, name="y%d" % t) for t in range(PACK)]
+        y_sb = [keep.tile([P, 2 * H if t < 2 else H], F32, name="y%d" % t) for t in range(PACK)]
         h_spare = [32, W - H + 32, W - H + 32, 32]
         h_half = [keep.tile([P, H + h_spare[m]], F32, name="h_half%d" % m) for m in range(4)]
 
@@ -61,10 +62,18 @@ def tile_picked_toketwghard_none_p_kernel(tc, x_words, x_scales, wa, tau, tau2, 
         nc.sync.dma_start(gate[:], gt.rearrange("(p t) o -> p (t o)", t=PACK))
         nc.sync.dma_start(w1_raw[1][:], w1_rows[:, :, HALF:])
         nc.sync.dma_start(n3_sb[:], n3)
-        for t in range(WHOLE_ROWS):
+        for t in range(2):
             nc.vector.memset(y_sb[t][:, H:], 0.0)
         for m in range(4):
             nc.vector.memset(h_half[m][:, H:], 0.0)
+
+        def interleave(on_scalar, grouped, planes):
+            target = grouped.rearrange("p (c i) t -> p c t i", i=RUN)
+            source = planes.rearrange("p t (c i) -> p c t i", i=RUN)
+            if on_scalar:
+                nc.scalar.activation(target, source, ACT.Copy)
+            else:
+                nc.vector.tensor_copy(target, source)
 
         def quantize(grouped, name):
             width = grouped.shape[1]
@@ -79,27 +88,39 @@ def tile_picked_toketwghard_none_p_kernel(tc, x_words, x_scales, wa, tau, tau2, 
         x_bytes = keep.tile([P, PACK, P], U8, name="x_bytes", align_bytes=64)
         wa_grouped = [keep.tile([P, HALF, PACK], BF16, name="wa_grouped%d" % c, tag="wa_grouped%d" % c, align_bytes=64) for c in range(2)]
         w1_grouped = keep.tile([P, N, PACK], BF16, name="w1_grouped", align_bytes=64)
-        nc.scalar.activation(wa_grouped[0][:], wa_raw[0][:].rearrange("p j w -> p w j"), ACT.Copy)
+        interleave(True, wa_grouped[0][:], wa_raw[0][:])
         nc.vector.tensor_copy(x_bytes[:].rearrange("p t m -> p m t"), scale_table[:].indirect(offs_sb[:]))
-        wa_mx = [quantize(wa_grouped[0], "wa0")]
-        nc.vector.tensor_copy(x_codes[:].rearrange("p t m -> p m t"), x_table[:].indirect(offs_sb[:]))
-        late = wa_raw[1][:].rearrange("p j w -> p w j")
-        nc.scalar.activation(wa_grouped[1][:, 0:P, :], late[:, 0:P, :], ACT.Copy)
-        nc.vector.tensor_copy(wa_grouped[1][:, P:, :], late[:, P:, :])
-        wa_mx.append(quantize(wa_grouped[1], "wa1"))
-        nc.scalar.activation(w1_grouped[:, 0:HALF, :], w1_raw[0][:].rearrange("p j w -> p w j"), ACT.Copy)
+        wa_codes = keep.tile([P, H], U32, name="wa_codes", align_bytes=64)
+        wa_scales = keep.tile([P, H], U8, name="wa_scales", align_bytes=64)
 
-        def project(acc, t, c):
+        def quantize_wa(c):
+            cols = slice(c * HALF, (c + 1) * HALF)
+            nc.vector.quantize_mx(
+                out=wa_codes[:, cols].bitcast(FP8X4),
+                scales=wa_scales[:, cols],
+                in_=wa_grouped[c][:].rearrange("p w j -> p (w j)"),
+            )
+
+        quantize_wa(0)
+        nc.vector.tensor_copy(x_codes[:].rearrange("p t m -> p m t"), x_table[:].indirect(offs_sb[:]))
+        interleave(True, wa_grouped[1][:, 0:QUARTER, :], wa_raw[1][:, :, 0:QUARTER])
+        interleave(False, wa_grouped[1][:, QUARTER:, :], wa_raw[1][:, :, QUARTER:])
+        quantize_wa(1)
+        interleave(True, w1_grouped[:, 0:HALF, :], w1_raw[0][:])
+
+        def project(acc, t, cols):
             nc.tensor.matmul_mx(
                 out=acc,
                 lhsT=x_codes[:, t, :].bitcast(FP8X4),
                 lhsT_scale=x_bytes[:, t, :],
-                rhs=wa_mx[c][0][:].bitcast(FP8X4),
-                rhs_scale=wa_mx[c][1][:],
+                rhs=wa_codes[:, cols].bitcast(FP8X4),
+                rhs_scale=wa_scales[:, cols],
                 start=True,
                 stop=True,
             )
 
+        gate3 = keep.tile([P, PACK], F32, name="gate3")
+        nc.gpsimd.tensor_scalar(gate3[:], gate[:], 3.0, 0.0, ALU.mult, ALU.add)
         bias = []
         for t in range(PACK):
             top = keep.tile([P, 1], F32, name="top%d" % t)
@@ -108,8 +129,8 @@ def tile_picked_toketwghard_none_p_kernel(tc, x_words, x_scales, wa, tau, tau2, 
                 early_top = keep.tile([P, 1], F32, name="early_top", tag="wa_grouped1", align_bytes=64)
                 early = psum.tile([P, HALF], F32, name="y_acc_early", tag="bank4")
                 acc = psum.tile([P, HALF], F32, name="y_acc0", tag="bank0")
-                project(early[:], 0, 0)
-                project(acc[:], 0, 1)
+                project(early[:], 0, slice(0, HALF))
+                project(acc[:], 0, slice(HALF, H))
                 nc.vector.tensor_scalar(
                     y_sb[0][:, 0:HALF], early[:], 1.0, None, ALU.mult, ALU.max, accum_out=early_top[:]
                 )
@@ -118,61 +139,94 @@ def tile_picked_toketwghard_none_p_kernel(tc, x_words, x_scales, wa, tau, tau2, 
                 )
             else:
                 acc = psum.tile([P, H], F32, name="y_acc%d" % t, tag="bank%d" % t)
-                for c in range(2):
-                    project(acc[:, c * HALF : (c + 1) * HALF], t, c)
+                project(acc[:], t, slice(0, H))
                 nc.vector.tensor_scalar(y_sb[t][:, 0:H], acc[:], 1.0, None, ALU.mult, ALU.max, accum_out=top[:])
             nc.gpsimd.tensor_scalar(bias_t[:], rates[:, :, t], top[:], -1.0, ALU.mult, ALU.mult)
             bias.append(bias_t)
 
-        gate3 = keep.tile([P, PACK], F32, name="gate3")
-        nc.gpsimd.tensor_scalar(gate3[:], gate[:], 3.0, 0.0, ALU.mult, ALU.add)
-        nc.vector.tensor_copy(w1_grouped[:, HALF:, :], w1_raw[1][:].rearrange("p j w -> p w j"))
+        nc.gpsimd.tensor_scalar(
+            w1_grouped[:, HALF:, :], w1_raw[1][:].rearrange("p j w -> p w j"), 1.0, 0.0, ALU.mult, ALU.add
+        )
         w1_codes, w1_scales = quantize(w1_grouped, "w1")
 
         z = keep.tile([P, 2, PACK, HALF], F32, name="z")
+        z_codes = [keep.tile([P, HALF], U32, name="z_codes%d" % c, align_bytes=64) for c in range(2)]
+        z_scales = [keep.tile([P, HALF], U8, name="z_scales%d" % c, align_bytes=64) for c in range(2)]
 
-        def make_z(t, first, width):
+        def exponentials(t, first, width, tag, scaled=None):
             entries = slice(first // STRIPE, (first + width) // STRIPE)
             label = "%d_%d" % (t, first)
-            both = keep.tile([P, 2, width], F32, name="exp" + label, tag="w1_raw0" if t == 0 else "exp" + label)
-            scaled_tag = {(2, HALF): "scaled3_0", (3, HALF): "z_grouped0"}.get((t, first), "scaled" + label)
-            scaled = keep.tile([P, width], F32, name="scaled" + label, tag=scaled_tag, align_bytes=64)
+            both = keep.tile([P, 2, width], F32, name="exp" + label, tag=tag)
+            if scaled is None:
+                scaled = keep.tile([P, width], F32, name="scaled" + label, tag="scaled", bufs=2)[:]
             for which, lists in ((1, n2_sb), (0, n1_sb)):
                 nc.scalar.activation(
                     both[:, which, :], y_sb[t][:].indirect(lists[:, entries]), ACT.Exp,
                     bias=bias[t][:, which : which + 1], scale=rates[:, which, t : t + 1],
                 )
-            nc.vector.tensor_scalar(scaled[:], both[:, 1, :], gate3[:, t : t + 1], None, ALU.mult)
+            nc.vector.tensor_scalar(scaled, both[:, 1, :], gate3[:, t : t + 1], None, ALU.mult)
+            return both, scaled
+
+        def difference(t, first, width, both, scaled):
+            run = min(width, HALF)
+            halves = slice(first // HALF, first // HALF + width // run)
             nc.vector.scalar_tensor_tensor(
-                z[:, first // HALF : (first + width) // HALF, t, :],
-                both[:, 0, :].rearrange("p (c j) -> p c j", j=HALF),
+                z[:, halves, t, first % HALF : first % HALF + run],
+                both[:, 0, :].rearrange("p (c j) -> p c j", j=run),
                 gate3[:, t : t + 1],
-                scaled[:].rearrange("p (c j) -> p c j", j=HALF),
+                scaled.rearrange("p (c j) -> p c j", j=run),
                 ALU.mult,
                 ALU.subtract,
             )
 
-        for t in range(WHOLE_ROWS):
-            make_z(t, 0, H)
+        def make_z(t, first, width, tag, scaled=None):
+            difference(t, first, width, *exponentials(t, first, width, tag, scaled))
+
+        def group_z(first, width):
+            grouped = keep.tile([P, width, PACK], BF16, name="z_grouped%d" % first, tag="z_grouped%d" % first, align_bytes=64)
+            interleave(False, grouped[:], z[:, first // HALF, :, first % HALF : first % HALF + width])
+            return grouped
+
+        def quantize_z(first, grouped):
+            cols = slice(first % HALF, first % HALF + grouped.shape[1])
+            nc.vector.quantize_mx(
+                out=z_codes[first // HALF][:, cols].bitcast(FP8X4),
+                scales=z_scales[first // HALF][:, cols],
+                in_=grouped[:].rearrange("p w j -> p (w j)"),
+            )
+
         h_acc = {}
-        for c in range(2):
-            for t in range(WHOLE_ROWS, PACK):
-                make_z(t, c * HALF, HALF)
-            z_grouped = keep.tile([P, HALF, PACK], BF16, name="z_grouped%d" % c, tag="z_grouped%d" % c, align_bytes=64)
-            nc.vector.tensor_copy(z_grouped[:], z[:, c, :, :].rearrange("p t j -> p j t"))
-            z_codes, z_scales = quantize(z_grouped, "z%d" % c)
+
+        def mix(c):
             for m in range(4):
                 acc = psum.tile([P, HALF], F32, name="h_acc%d_%d" % (c, m), tag="bank%d" % ((5 + 4 * c + m) % 8))
                 nc.tensor.matmul_mx(
                     out=acc[:],
                     lhsT=w1_codes[:, m * P : (m + 1) * P].bitcast(FP8X4),
                     lhsT_scale=w1_scales[:, m * P : (m + 1) * P],
-                    rhs=z_codes[:].bitcast(FP8X4),
-                    rhs_scale=z_scales[:],
+                    rhs=z_codes[c][:].bitcast(FP8X4),
+                    rhs_scale=z_scales[c][:],
                     start=True,
                     stop=True,
                 )
                 h_acc[c, m] = acc
+
+        make_z(0, 0, H, "w1_raw0")
+        make_z(1, 0, H, "exp1")
+        for t in range(2, PACK):
+            make_z(t, 0, HALF, "exp%d" % t)
+        quantize_z(0, group_z(0, HALF))
+        mix(0)
+        third, fourth = HALF, HALF + QUARTER
+        make_z(2, HALF, HALF, "exp1")
+        late_scaled = keep.tile([P, 2, QUARTER], F32, name="late_scaled", tag="z_grouped0", align_bytes=64)
+        make_z(3, third, QUARTER, "exp2", late_scaled[:, 0, :])
+        last = exponentials(3, fourth, QUARTER, "exp3", late_scaled[:, 1, :])
+        third_grouped = group_z(third, QUARTER)
+        difference(PACK - 1, fourth, QUARTER, *last)
+        quantize_z(third, third_grouped)
+        quantize_z(fourth, group_z(fourth, QUARTER))
+        mix(1)
 
         def leave_psum(on_scalar, c, m):
             target = h_half[m][:, c * HALF : (c + 1) * HALF]

from contextlib import ExitStack

import concourse.mybir as mybir

K, T, S, N, H, W = 512, 2048, 512, 512, 512, 1024
FLOPS = 2 * K * S * H + 2 * S * N * H

F32 = mybir.dt.float32
BF16 = mybir.dt.bfloat16
I32 = mybir.dt.int32
U32 = mybir.dt.uint32
U16 = mybir.dt.uint16
U8 = mybir.dt.uint8
FP8X4 = mybir.dt.float8_e4m3fn_x4
ALU = mybir.AluOpType
ACT = mybir.ActivationFunctionType

P = 128
PACK = 4
STRIPE = 16
HALF = 256
QUARTER = 128
RUN = 4


def tile_picked_toketwghard_none_p_kernel(tc, x_words, x_scales, wa, tau, tau2, gt, w1, offs, n1, n2, n3, out):
    nc = tc.nc
    with ExitStack() as ctx:
        keep = ctx.enter_context(tc.tile_pool(name="keep", bufs=1))
        psum = ctx.enter_context(tc.psum_pool(name="psum", bufs=1))

        offs_sb = keep.tile([P, S // STRIPE], U16, name="offs_sb")
        n1_sb = keep.tile([P, H // STRIPE], U16, name="n1_sb")
        n2_sb = keep.tile([P, H // STRIPE], U16, name="n2_sb")
        n3_sb = keep.tile([P, W // STRIPE], U16, name="n3_sb")
        x_table = keep.tile([P, T], U32, name="x_table")
        scale_table = keep.tile([P, T], U8, name="scale_table")
        wa_raw = [keep.tile([P, PACK, HALF], F32, name="wa_raw%d" % c) for c in range(2)]
        w1_raw = [keep.tile([P, PACK, HALF], F32, name="w1_raw%d" % c, tag="w1_raw%d" % c) for c in range(2)]
        rates = keep.tile([P, 2, 8], F32, name="rates")
        gate = keep.tile([P, PACK], F32, name="gate")
        y_sb = [keep.tile([P, 2 * H if t < 2 else H], F32, name="y%d" % t) for t in range(PACK)]
        h_spare = [32, W - H + 32, W - H + 32, 32]
        h_half = [keep.tile([P, H + h_spare[m]], F32, name="h_half%d" % m) for m in range(4)]

        wa_rows = wa.rearrange("(p j) w -> p j w", j=PACK)
        w1_rows = w1.rearrange("(p j) w -> p j w", j=PACK)
        nc.vector.memset(scale_table[:].bitcast(I32), 0)
        nc.sync.dma_start(offs_sb[:], offs)
        nc.sync.dma_start(wa_raw[0][:], wa_rows[:, :, 0:HALF])
        for q in range(4):
            nc.sync.dma_start(
                scale_table[32 * q : 32 * q + 4, :].bitcast(I32), x_scales[0, 4 * q : 4 * q + 4, :].bitcast(I32)
            )
        nc.sync.dma_start(x_table[:].bitcast(I32), x_words[0].rearrange("p c r -> p (c r)").bitcast(I32))
        nc.sync.dma_start(wa_raw[1][:], wa_rows[:, :, HALF:])
        nc.sync.dma_start(w1_raw[0][:], w1_rows[:, :, 0:HALF])
        nc.sync.dma_start(n2_sb[:], n2)
        nc.sync.dma_start(n1_sb[:], n1)
        nc.sync.dma_start(rates[:, 1, 0:PACK], tau2.rearrange("(p t) o -> p (t o)", t=PACK))
        nc.sync.dma_start(rates[:, 0, 0:PACK], tau.rearrange("(p t) o -> p (t o)", t=PACK))
        nc.sync.dma_start(gate[:], gt.rearrange("(p t) o -> p (t o)", t=PACK))
        nc.sync.dma_start(w1_raw[1][:], w1_rows[:, :, HALF:])
        nc.sync.dma_start(n3_sb[:], n3)
        for t in range(2):
            nc.vector.memset(y_sb[t][:, H:], 0.0)
        for m in range(4):
            nc.vector.memset(h_half[m][:, H:], 0.0)

        def interleave(on_scalar, grouped, planes):
            target = grouped.rearrange("p (c i) t -> p c t i", i=RUN)
            source = planes.rearrange("p t (c i) -> p c t i", i=RUN)
            if on_scalar:
                nc.scalar.activation(target, source, ACT.Copy)
            else:
                nc.vector.tensor_copy(target, source)

        def quantize(grouped, name):
            width = grouped.shape[1]
            codes = keep.tile([P, width], U32, name=name + "_codes", align_bytes=64)
            scales = keep.tile([P, width], U8, name=name + "_scales", align_bytes=64)
            nc.vector.quantize_mx(
                out=codes[:].bitcast(FP8X4), scales=scales[:], in_=grouped[:].rearrange("p w j -> p (w j)")
            )
            return codes, scales

        x_codes = keep.tile([P, PACK, P], U32, name="x_codes", align_bytes=64)
        x_bytes = keep.tile([P, PACK, P], U8, name="x_bytes", align_bytes=64)
        wa_grouped = [keep.tile([P, HALF, PACK], BF16, name="wa_grouped%d" % c, tag="wa_grouped%d" % c, align_bytes=64) for c in range(2)]
        w1_grouped = keep.tile([P, N, PACK], BF16, name="w1_grouped", align_bytes=64)
        interleave(True, wa_grouped[0][:], wa_raw[0][:])
        nc.vector.tensor_copy(x_bytes[:].rearrange("p t m -> p m t"), scale_table[:].indirect(offs_sb[:]))
        wa_codes = keep.tile([P, H], U32, name="wa_codes", align_bytes=64)
        wa_scales = keep.tile([P, H], U8, name="wa_scales", align_bytes=64)

        def quantize_wa(c):
            cols = slice(c * HALF, (c + 1) * HALF)
            nc.vector.quantize_mx(
                out=wa_codes[:, cols].bitcast(FP8X4),
                scales=wa_scales[:, cols],
                in_=wa_grouped[c][:].rearrange("p w j -> p (w j)"),
            )

        quantize_wa(0)
        nc.vector.tensor_copy(x_codes[:].rearrange("p t m -> p m t"), x_table[:].indirect(offs_sb[:]))
        interleave(True, wa_grouped[1][:, 0:QUARTER, :], wa_raw[1][:, :, 0:QUARTER])
        interleave(False, wa_grouped[1][:, QUARTER:, :], wa_raw[1][:, :, QUARTER:])
        quantize_wa(1)
        interleave(True, w1_grouped[:, 0:HALF, :], w1_raw[0][:])

        def project(acc, t, cols):
            nc.tensor.matmul_mx(
                out=acc,
                lhsT=x_codes[:, t, :].bitcast(FP8X4),
                lhsT_scale=x_bytes[:, t, :],
                rhs=wa_codes[:, cols].bitcast(FP8X4),
                rhs_scale=wa_scales[:, cols],
                start=True,
                stop=True,
            )

        gate3 = keep.tile([P, PACK], F32, name="gate3")
        nc.gpsimd.tensor_scalar(gate3[:], gate[:], 3.0, 0.0, ALU.mult, ALU.add)
        bias = []
        for t in range(PACK):
            top = keep.tile([P, 1], F32, name="top%d" % t)
            bias_t = keep.tile([P, 2], F32, name="bias%d" % t)
            if t == 0:
                early_top = keep.tile([P, 1], F32, name="early_top", tag="wa_grouped1", align_bytes=64)
                early = psum.tile([P, HALF], F32, name="y_acc_early", tag="bank4")
                acc = psum.tile([P, HALF], F32, name="y_acc0", tag="bank0")
                project(early[:], 0, slice(0, HALF))
                project(acc[:], 0, slice(HALF, H))
                nc.vector.tensor_scalar(
                    y_sb[0][:, 0:HALF], early[:], 1.0, None, ALU.mult, ALU.max, accum_out=early_top[:]
                )
                nc.vector.tensor_scalar(
                    y_sb[0][:, HALF:H], acc[:], 1.0, early_top[:], ALU.mult, ALU.max, accum_out=top[:]
                )
            else:
                acc = psum.tile([P, H], F32, name="y_acc%d" % t, tag="bank%d" % t)
                project(acc[:], t, slice(0, H))
                nc.vector.tensor_scalar(y_sb[t][:, 0:H], acc[:], 1.0, None, ALU.mult, ALU.max, accum_out=top[:])
            nc.gpsimd.tensor_scalar(bias_t[:], rates[:, :, t], top[:], -1.0, ALU.mult, ALU.mult)
            bias.append(bias_t)

        nc.gpsimd.tensor_scalar(
            w1_grouped[:, HALF:, :], w1_raw[1][:].rearrange("p j w -> p w j"), 1.0, 0.0, ALU.mult, ALU.add
        )
        w1_codes, w1_scales = quantize(w1_grouped, "w1")

        z = keep.tile([P, 2, PACK, HALF], F32, name="z")
        z_codes = [keep.tile([P, HALF], U32, name="z_codes%d" % c, align_bytes=64) for c in range(2)]
        z_scales = [keep.tile([P, HALF], U8, name="z_scales%d" % c, align_bytes=64) for c in range(2)]

        def exponentials(t, first, width, tag, scaled=None):
            entries = slice(first // STRIPE, (first + width) // STRIPE)
            label = "%d_%d" % (t, first)
            both = keep.tile([P, 2, width], F32, name="exp" + label, tag=tag)
            if scaled is None:
                scaled = keep.tile([P, width], F32, name="scaled" + label, tag="scaled", bufs=2)[:]
            for which, lists in ((1, n2_sb), (0, n1_sb)):
                nc.scalar.activation(
                    both[:, which, :], y_sb[t][:].indirect(lists[:, entries]), ACT.Exp,
                    bias=bias[t][:, which : which + 1], scale=rates[:, which, t : t + 1],
                )
            nc.vector.tensor_scalar(scaled, both[:, 1, :], gate3[:, t : t + 1], None, ALU.mult)
            return both, scaled

        def difference(t, first, width, both, scaled):
            run = min(width, HALF)
            halves = slice(first // HALF, first // HALF + width // run)
            nc.vector.scalar_tensor_tensor(
                z[:, halves, t, first % HALF : first % HALF + run],
                both[:, 0, :].rearrange("p (c j) -> p c j", j=run),
                gate3[:, t : t + 1],
                scaled.rearrange("p (c j) -> p c j", j=run),
                ALU.mult,
                ALU.subtract,
            )

        def make_z(t, first, width, tag, scaled=None):
            difference(t, first, width, *exponentials(t, first, width, tag, scaled))

        def group_z(first, width):
            grouped = keep.tile([P, width, PACK], BF16, name="z_grouped%d" % first, tag="z_grouped%d" % first, align_bytes=64)
            interleave(False, grouped[:], z[:, first // HALF, :, first % HALF : first % HALF + width])
            return grouped

        def quantize_z(first, grouped):
            cols = slice(first % HALF, first % HALF + grouped.shape[1])
            nc.vector.quantize_mx(
                out=z_codes[first // HALF][:, cols].bitcast(FP8X4),
                scales=z_scales[first // HALF][:, cols],
                in_=grouped[:].rearrange("p w j -> p (w j)"),
            )

        h_acc = {}

        def mix(c):
            for m in range(4):
                acc = psum.tile([P, HALF], F32, name="h_acc%d_%d" % (c, m), tag="bank%d" % ((5 + 4 * c + m) % 8))
                nc.tensor.matmul_mx(
                    out=acc[:],
                    lhsT=w1_codes[:, m * P : (m + 1) * P].bitcast(FP8X4),
                    lhsT_scale=w1_scales[:, m * P : (m + 1) * P],
                    rhs=z_codes[c][:].bitcast(FP8X4),
                    rhs_scale=z_scales[c][:],
                    start=True,
                    stop=True,
                )
                h_acc[c, m] = acc

        make_z(0, 0, H, "w1_raw0")
        make_z(1, 0, H, "exp1")
        for t in range(2, PACK):
            make_z(t, 0, HALF, "exp%d" % t)
        quantize_z(0, group_z(0, HALF))
        mix(0)
        third, fourth = HALF, HALF + QUARTER
        make_z(2, HALF, HALF, "exp1")
        late_scaled = keep.tile([P, 2, QUARTER], F32, name="late_scaled", tag="z_grouped0", align_bytes=64)
        make_z(3, third, QUARTER, "exp2", late_scaled[:, 0, :])
        last = exponentials(3, fourth, QUARTER, "exp3", late_scaled[:, 1, :])
        third_grouped = group_z(third, QUARTER)
        difference(PACK - 1, fourth, QUARTER, *last)
        quantize_z(third, third_grouped)
        quantize_z(fourth, group_z(fourth, QUARTER))
        mix(1)

        def leave_psum(on_scalar, c, m):
            target = h_half[m][:, c * HALF : (c + 1) * HALF]
            if on_scalar:
                nc.scalar.activation(target, h_acc[c, m][:], ACT.Copy, scale=0.5)
            else:
                nc.vector.tensor_scalar(target, h_acc[c, m][:], 0.5, None, ALU.mult)

        members = [keep.tile([P, H, 2], F32, name="members%d" % m) for m in range(4)]
        larger = [keep.tile([P, H], F32, name="larger%d" % m) for m in range(4)]
        smaller = [keep.tile([P, H], F32, name="smaller%d" % m) for m in range(4)]
        gap = [keep.tile([P, H], F32, name="gap%d" % m) for m in range(4)]
        curve = [keep.tile([P, H], F32, name="curve%d" % m) for m in range(4)]
        result = [keep.tile([P, H], F32, name="result%d" % m) for m in range(4)]

        def fetch(on_scalar, m, cols):
            window = h_half[m][:].indirect(n3_sb[:, 2 * cols.start // STRIPE : 2 * cols.stop // STRIPE])
            flat = members[m][:, cols, :].rearrange("p j e -> p (j e)")
            if on_scalar:
                nc.scalar.activation(flat, window, ACT.Copy)
            else:
                nc.vector.tensor_copy(flat, window)

        def compare(m, cols):
            pair = members[m]
            nc.vector.tensor_tensor(smaller[m][:, cols], pair[:, cols, 0], pair[:, cols, 1], ALU.min)
            nc.vector.tensor_tensor(larger[m][:, cols], pair[:, cols, 0], pair[:, cols, 1], ALU.max)
            nc.vector.tensor_tensor(gap[m][:, cols], h_half[m][:, cols], smaller[m][:, cols], ALU.subtract)

        def bend(m, cols):
            nc.scalar.activation(curve[m][:, cols], larger[m][:, cols], ACT.Tanh)

        def finish(m, cols):
            nc.vector.scalar_tensor_tensor(
                result[m][:, cols], curve[m][:, cols], 1.0, gap[m][:, cols], ALU.add, ALU.mult
            )
            nc.sync.dma_start(out[m * P : (m + 1) * P, cols], result[m][:, cols])

        left, right, whole = slice(0, HALF), slice(HALF, H), slice(0, H)
        for m in range(4):
            leave_psum(True, 0, m)
        leave_psum(False, 1, 0)
        leave_psum(True, 1, 1)
        fetch(False, 0, left)
        fetch(True, 0, right)
        fetch(True, 1, whole)
        leave_psum(False, 1, 2)
        leave_psum(False, 1, 3)
        fetch(True, 2, whole)
        compare(0, whole)
        bend(0, whole)
        fetch(True, 3, left)
        fetch(True, 3, right)
        compare(1, whole)
        bend(1, whole)
        compare(2, whole)
        bend(2, whole)
        finish(0, whole)
        compare(3, left)
        bend(3, left)
        compare(3, right)
        bend(3, right)
        finish(1, whole)
        finish(2, whole)
        finish(3, left)
        finish(3, right)
